import numpy as np
import ml_dtypes


def mxq(x, axis, fmt="e4m3"):
    dtype, down = {"e4m3": (ml_dtypes.float8_e4m3fn, 7), "e5m2": (ml_dtypes.float8_e5m2, 14)}[fmt]
    v = np.moveaxis(np.asarray(x, np.float32).astype(ml_dtypes.bfloat16).astype(np.float64), axis, -1)
    blocks = v.reshape(v.shape[:-1] + (-1, 32))
    amax = np.abs(blocks).max(-1, keepdims=True)
    byte = np.maximum(np.where(amax > 0, np.frexp(amax)[1] - 1 + 127, 0) - down, 1)
    scale = np.exp2(byte - 127.0)
    codes = (blocks / scale).astype(np.float32).astype(dtype).astype(np.float64)
    return np.moveaxis((codes * scale).reshape(v.shape), -1, axis)


WIDE = False


def mx_kscale(k):
    if not WIDE:
        return np.ones(k)
    levels = np.array([24, -24, 12, -12, 0])
    if k % 512:
        return np.exp2(np.random.permutation(np.resize(levels, k // 32))).repeat(32)
    a = np.empty((k // 512, 16))
    for p in range(k // 512):
        a[p, :8] = np.random.permutation(np.resize(levels, 8))
        for g in range(8):
            far = levels[np.abs(levels - a[p, g]) >= 10]
            a[p, g + 8] = far[np.random.randint(len(far))]
    return np.exp2(a.ravel()).repeat(32)


def f64(x):
    return np.asarray(x).astype(np.float64)


def striped8(idx):
    return np.concatenate([v.reshape(-1, 16).T for v in idx]).astype(np.uint16)


def unstriped8(offs):
    return np.stack([offs[16 * g:16 * g + 16].T.reshape(-1) for g in range(8)]).astype(np.int64)


E2M1 = np.array([0.0, 0.5, 1.0, 1.5, 2.0, 3.0, 4.0, 6.0, -0.0, -0.5, -1.0, -1.5, -2.0, -3.0, -4.0, -6.0])


def pack_weight(w, fmt):
    k, n = w.shape
    w = f64(np.asarray(w, np.float32).astype(ml_dtypes.bfloat16)).reshape(k // 32, 32, n)
    amax = np.abs(w).max(1)
    if fmt == "e4m3":
        byte = np.frexp(amax)[1] - 1 + 127 - 7
    else:
        mant, ex = np.frexp(amax / 6.0)
        byte = np.where(mant > 0.5, ex, ex - 1) + 127
    byte = np.clip(np.where(amax > 0, byte, 1), 1, 254)
    scaled = (w * np.exp2(127.0 - byte)[:, None, :]).reshape(k, n).astype(np.float32)
    by_word = np.ascontiguousarray(scaled.reshape(k // 512, 128, 4, n).transpose(0, 1, 3, 2))
    if fmt == "e4m3":
        words = by_word.astype(ml_dtypes.float8_e4m3fn).view(np.uint8)
    else:
        c = by_word.astype(ml_dtypes.float4_e2m1fn).view(np.uint8) & 0xF
        words = (c[..., 0::2] | (c[..., 1::2] << 4)).reshape(k // 512, 128, 2 * n)
    return np.ascontiguousarray(words), np.ascontiguousarray(byte.astype(np.uint8).reshape(k // 512, 16, n))


def unpack_weight(words, scales, fmt):
    g, _, n = scales.shape
    words = np.ascontiguousarray(words).reshape(g, 128, n, -1)
    if fmt == "e4m3":
        vals = words.view(ml_dtypes.float8_e4m3fn).astype(np.float64)
    else:
        nib = np.empty((g, 128, n, 4), np.uint8)
        nib[..., 0::2] = words & 0xF
        nib[..., 1::2] = words >> 4
        vals = E2M1[nib]
    vals = vals * np.repeat(np.exp2(scales.astype(np.float64) - 127.0), 8, axis=1)[..., None]
    return vals.transpose(0, 1, 3, 2).reshape(g * 512, n)


def silu(f):
    return f / (1.0 + np.exp(-np.maximum(f, -700.0)))


K, R, N, T, J = 1024, 512, 512, 2048, 1024


def setup_inputs():
    n = np.random.standard_normal
    s = mx_kscale(K)[:, None]
    u = mx_kscale(R)[:, None]
    p_wg = pack_weight(n((K, R)) / np.sqrt(K) / s, "e2m1")
    p_wu = pack_weight(n((K, R)) / np.sqrt(K) / s * u.T, "e2m1")
    p_wd = pack_weight(n((R, N)) / np.sqrt(R) / u, "e2m1")
    return {
        "xT": (n((K, T)) * s).astype(np.float32),
        "wgt": np.repeat(np.random.uniform(0.5, 2.0, (8, J)), 16, axis=0).astype(np.float32),
        "wg_words": p_wg[0],
        "wg_scales": p_wg[1],
        "wu_words": p_wu[0],
        "wu_scales": p_wu[1],
        "wd_words": p_wd[0],
        "wd_scales": p_wd[1],
        "b": (0.3 * n(N)).astype(np.float32),
        "offs": striped8(np.stack([np.random.permutation(T)[:J] for _ in range(8)])),
    }


def reference(xT, wgt, wg_words, wg_scales, wu_words, wu_scales, wd_words, wd_scales, b, offs):
    idx = unstriped8(offs)
    rows = np.arange(K)
    xg = f64(wgt)[rows // 4 % 128] * f64(xT)[rows[:, None], idx[rows % 512 // 64]]
    xT_ = mxq(xg, 0, "e4m3")
    wg_ = unpack_weight(wg_words, wg_scales, "e2m1")
    wu_ = unpack_weight(wu_words, wu_scales, "e2m1")
    ga = wg_.T @ xT_
    ub = wu_.T @ xT_
    h = silu(ga) * ub
    h_ = mxq(h, 0, "e4m3")
    wd_ = unpack_weight(wd_words, wd_scales, "e2m1")
    y = wd_.T @ h_
    return y + f64(b)[:, None]

@@ -1,0 +1,367 @@
+from contextlib import ExitStack
+
+import concourse.mybir as mybir
+
+K, R, N, T, J = 1024, 512, 512, 2048, 1024
+FLOPS = 2 * (2 * K * R + R * N) * J
+
+F32 = mybir.dt.float32
+BF16 = mybir.dt.bfloat16
+I32 = mybir.dt.int32
+U32 = mybir.dt.uint32
+U16 = mybir.dt.uint16
+U8 = mybir.dt.uint8
+FP8X4 = mybir.dt.float8_e4m3fn_x4
+FP4X4 = mybir.dt.float4_e2m1fn_x4
+ACT = mybir.ActivationFunctionType
+ALU = mybir.AluOpType
+
+P = 128
+PLAN = [
+    ('G', 0, 0, 512),
+    ('G', 0, 512, 1024),
+    ('G', 1, 0, 512),
+    ('I', 0, 0, 512, 'S'),
+    ('G', 1, 512, 1024),
+    ('I', 0, 512, 1024, 'S'),
+    ('G', 2, 0, 512),
+    ('G', 2, 512, 1024),
+    ('G', 3, 0, 512),
+    ('I', 1, 0, 512, 'S'),
+    ('G', 3, 512, 1024),
+    ('I', 1, 512, 1024, 'S'),
+    ('G', 4, 0, 512),
+    ('G', 4, 512, 1024),
+    ('G', 5, 0, 512),
+    ('I', 2, 0, 512, 'S'),
+    ('G', 5, 512, 1024),
+    ('I', 2, 512, 1024, 'S'),
+    ('G', 7, 0, 128),
+    ('G', 6, 0, 512),
+    ('G', 7, 128, 256),
+    ('I', 3, 128, 256, 'S'),
+    ('G', 7, 256, 512),
+    ('Q', 0, 0, 512),
+    ('Q', 1, 128, 256),
+    ('I', 3, 256, 512, 'S'),
+    ('g', 0, 1, 0, 0),
+    ('g', 0, 3, 0, 6),
+    ('I', 3, 0, 128, 'S'),
+    ('Q', 1, 0, 128),
+    ('Q', 1, 256, 512),
+    ('g', 0, 0, 0, 7),
+    ('g', 0, 3, 1, 3),
+    ('g', 0, 0, 1, 0),
+    ('g', 0, 1, 1, 1),
+    ('s', 0, 0, 256, 512),
+    ('g', 0, 2, 0, 3),
+    ('G', 6, 512, 768),
+    ('Q', 0, 512, 1024),
+    ('s', 0, 0, 0, 256),
+    ('g', 0, 2, 1, 2),
+    ('u', 2, 7),
+    ('G', 7, 768, 1024),
+    ('s', 0, 2, 0, 256),
+    ('u', 1, 5),
+    ('s', 0, 3, 0, 256),
+    ('s', 0, 2, 256, 512),
+    ('s', 0, 1, 0, 256),
+    ('m', 1),
+    ('s', 0, 1, 256, 512),
+    ('g', 1, 3, 0, 5),
+    ('G', 7, 512, 768),
+    ('u', 0, 4),
+    ('I', 3, 512, 768, 'V'),
+    ('s', 0, 3, 256, 512),
+    ('m', 0),
+    ('G', 6, 768, 1024),
+    ('u', 3, 2),
+    ('I', 3, 768, 1024, 'S'),
+    ('Q', 1, 768, 1024),
+    ('g', 1, 2, 0, 1),
+    ('m', 2),
+    ('g', 1, 1, 0, 3),
+    ('g', 1, 0, 0, 0),
+    ('qh', 0, 256),
+    ('Q', 1, 512, 768),
+    ('g', 1, 3, 1, 3),
+    ('m', 3),
+    ('s', 1, 3, 512, 1024),
+    ('qh', 256, 512),
+    ('y', 0, 256, (0, 1), 7),
+    ('g', 1, 2, 1, 2),
+    ('b', 0, (0, 1), 'S'),
+    ('y', 256, 512, (2, 3), 2),
+    ('g', 1, 0, 1, 4),
+    ('g', 1, 1, 1, 5),
+    ('b', 256, (2, 3), 'S'),
+    ('s', 1, 2, 512, 1024),
+    ('s', 1, 0, 512, 1024),
+    ('y', 0, 256, (2, 3), 4),
+    ('u', 4, 1),
+    ('u', 7, 6),
+    ('s', 1, 1, 512, 1024),
+    ('m', 4),
+    ('m', 7),
+    ('y', 256, 512, (0, 1), 7),
+    ('u', 5, 5),
+    ('b', 0, (2, 3), 'S'),
+    ('m', 5),
+    ('qh', 896, 1024),
+    ('u', 6, 0),
+    ('y', 896, 1024, (2, 3), 1),
+    ('b', 256, (0, 1), 'S'),
+    ('st', 256, 512, (0, 1, 2, 3)),
+    ('m', 6),
+    ('qh', 768, 896),
+    ('b', 896, (2, 3), 'S'),
+    ('qh', 512, 768),
+    ('st', 896, 1024, (2, 3)),
+    ('y', 768, 896, (0, 1, 2, 3), 4),
+    ('b', 768, (0, 1, 2, 3), 'V'),
+    ('y', 512, 768, (0, 1), 6),
+    ('b', 512, (0, 1), 'S'),
+    ('y', 896, 1024, (0, 1), 3),
+    ('b', 896, (0, 1), 'S'),
+    ('y', 512, 768, (2, 3), 7),
+    ('b', 512, (2, 3), 'V'),
+    ('st', 768, 896, (0, 1, 2, 3)),
+    ('st', 0, 256, (0, 1, 2, 3)),
+    ('st', 512, 768, (0, 1, 2, 3)),
+    ('st', 896, 1024, (0, 1)),
+]
+SHARES = {"x_codes0_0": "plane5", "x_codes0_512": "x_bf1_256", "picked3_512": "x_bf1_128", "picked3_768": "x_bf1_0"}
+STRETCHES = ((0, 128), (128, 256), (256, 512), (512, 768), (768, 1024))
+
+
+def tile_list_silu_bias_kernel(
+    tc, xT, wgt, wg_words, wg_scales, wu_words, wu_scales, wd_words, wd_scales, b, offs, out
+):
+    nc = tc.nc
+    with ExitStack() as ctx:
+        keep = ctx.enter_context(tc.tile_pool(name="keep", bufs=1))
+        psum = ctx.enter_context(tc.psum_pool(name="psum", bufs=1))
+
+        offsets = keep.tile([P, J // 16], U16, name="offsets")
+        w_raw = keep.tile([P, 4, 1024], U8, name="w_raw", align_bytes=64)
+        s_raw = [keep.tile([P, 2, 512], U8, name="s_raw%d" % w, align_bytes=64) for w in range(2)]
+        w_perm = keep.tile([P, 4, 4, 256], U8, name="w_perm", align_bytes=64)
+        s_perm = keep.tile([P, 4, 4, 128], U8, name="s_perm", align_bytes=64)
+        wd_sb = keep.tile([P, 1024], U8, name="wd_sb", align_bytes=64)
+        sd_sb = keep.tile([P, 512], U8, name="sd_sb", align_bytes=64)
+        b_sb = keep.tile([P, 4], F32, name="b_sb")
+        made = {}
+
+        def tile_of(name, shape, dtype):
+            if name not in made:
+                made[name] = keep.tile(shape, dtype, name=name, tag=SHARES.get(name, name), align_bytes=64)
+            return made[name]
+
+        wgt_sb = [tile_of("wgt%d" % h, [P, 512], F32) for h in range(2)]
+        planes = [tile_of("plane%d" % q, [P, T], F32) for q in range(8)]
+
+        def picked(pair, j0, j1):
+            lo, hi = (j0 // 512 * 512, j0 // 512 * 512 + 512)
+            if pair == 3 and j0 >= 512:
+                lo, hi = (j0 // 256 * 256, j0 // 256 * 256 + 256)
+            return tile_of("picked%d_%d" % (pair, lo), [P, 2, hi - lo], F32)[:, :, j0 - lo : j1 - lo]
+
+        def x_bf(a, j0, j1):
+            lo, hi = (j0 // 512 * 512, j0 // 512 * 512 + 512)
+            if a == 1:
+                lo, hi = [s for s in STRETCHES if s[0] <= j0 < s[1]][0]
+            return tile_of("x_bf%d_%d" % (a, lo), [P, hi - lo, 4], BF16)[:, j0 - lo : j1 - lo, :]
+
+        def x_codes(a, j0, j1):
+            lo = j0 // 512 * 512
+            return tile_of("x_codes%d_%d" % (a, lo), [P, 512], U32)[:, j0 - lo : j1 - lo]
+
+        def x_scales(a, j0, j1):
+            lo = j0 // 512 * 512
+            return tile_of("x_scales%d_%d" % (a, lo), [P, 512], U8)[:, j0 - lo : j1 - lo]
+
+        gate = keep.tile([P, 8, 4, 128], F32, name="gate")
+        h_bf = keep.tile([P, J, 4], BF16, name="h_bf", align_bytes=64)
+        h_codes = keep.tile([P, J], U32, name="h_codes", align_bytes=64)
+        h_scales = keep.tile([P, J], U8, name="h_scales", align_bytes=64)
+        y_sb = {}
+        warm = keep.tile([P, 2], F32, name="warm")
+
+        nc.vector.memset(s_raw[0][:].rearrange("p a n -> p (a n)").bitcast(I32), 0)
+        nc.vector.memset(s_raw[1][:].rearrange("p a n -> p (a n)").bitcast(I32), 0)
+        nc.vector.memset(sd_sb[:].bitcast(I32), 0)
+        nc.vector.memset(warm[:, 0:1], 0.0)
+        nc.scalar.activation(warm[:, 1:2], warm[:, 0:1], ACT.Silu)
+
+        def load_words(w, words):
+            nc.sync.dma_start(
+                out=w_raw[:, 2 * w : 2 * w + 2, :].bitcast(I32),
+                in_=words.rearrange("a p n -> p a n").bitcast(I32),
+            )
+
+        def load_scales(dst, scales):
+            for q in range(4):
+                nc.sync.dma_start(
+                    out=dst[32 * q : 32 * q + 4].bitcast(I32),
+                    in_=scales[:, 4 * q : 4 * q + 4, :].rearrange("a r n -> r a n").bitcast(I32),
+                )
+
+        def load_plane(q):
+            a, i = divmod(q, 4)
+            rows = xT[512 * a : 512 * a + 512, :].rearrange("(p i) t -> p i t", i=4)
+            nc.sync.dma_start(out=planes[q][:], in_=rows[:, i, :])
+
+        def permute_words(w):
+            nc.vector.tensor_copy(
+                out=w_perm[:, 2 * w : 2 * w + 2].bitcast(U16),
+                in_=w_raw[:, 2 * w : 2 * w + 2, :].bitcast(U16).rearrange("p a (m t) -> p a t m", t=4),
+            )
+
+        def permute_scales(w):
+            nc.vector.tensor_copy(
+                out=s_perm[:, 2 * w : 2 * w + 2],
+                in_=s_raw[w][:].rearrange("p a (m t) -> p a t m", t=4),
+            )
+
+        nc.sync.dma_start(offsets[:], offs)
+        load_words(0, wg_words)
+        load_words(1, wu_words)
+        load_scales(s_raw[0], wg_scales)
+        nc.sync.dma_start(out=wgt_sb[0][:], in_=wgt[:, 0:512])
+        load_plane(0)
+        load_scales(s_raw[1], wu_scales)
+        nc.sync.dma_start(out=wgt_sb[1][:], in_=wgt[:, 512:1024])
+        for q in range(1, 8):
+            load_plane(q)
+        nc.sync.dma_start(out=wd_sb[:].bitcast(I32), in_=wd_words[0].bitcast(I32))
+        for q in range(4):
+            nc.sync.dma_start(
+                out=sd_sb[32 * q : 32 * q + 4, :].bitcast(I32),
+                in_=wd_scales[0, 4 * q : 4 * q + 4, :].bitcast(I32),
+            )
+        with nc.allow_non_contiguous_dma(reason="one bias value a partition"):
+            nc.sync.dma_start(out=b_sb[:], in_=b.rearrange("(c p) -> p c", p=P))
+
+        permute_words(0)
+        permute_words(1)
+        permute_scales(0)
+        permute_scales(1)
+
+        def bank_tile(bank):
+            return psum.tile([P, 512], F32, name="bank%d" % bank)
+
+        def first_layer_pass(dst, w, a, t, cols):
+            nc.tensor.matmul_mx(
+                out=dst,
+                lhsT=w_perm[:, 2 * w + a, t, :].bitcast(FP4X4),
+                lhsT_scale=s_perm[:, 2 * w + a, t, :],
+                rhs=x_codes(a, cols.start, cols.stop).bitcast(FP8X4),
+                rhs_scale=x_scales(a, cols.start, cols.stop),
+                start=(a == 0),
+                stop=(a == 1),
+            )
+
+        out_v = out.rearrange("(c p) j -> p c j", p=P)
+        held = {}
+        for step in PLAN:
+            kind = step[0]
+            if kind == "G":
+                q, j0, j1 = step[1:]
+                nc.vector.tensor_tensor(
+                    picked(q // 2, j0, j1)[:, q % 2, :],
+                    planes[q][:].indirect(offsets[:, j0 // 16 : j1 // 16]),
+                    wgt_sb[j0 // 512][:, j0 % 512 : j0 % 512 + j1 - j0],
+                    ALU.mult,
+                )
+            elif kind == "I":
+                pair, j0, j1, eng = step[1:]
+                a, e = divmod(pair, 2)
+                parts = [s for s in STRETCHES if j0 <= s[0] < j1] if a == 1 else [(j0, j1)]
+                for lo, hi in parts:
+                    dst = x_bf(a, lo, hi)[:, :, 2 * e : 2 * e + 2]
+                    src = picked(pair, lo, hi).rearrange("p e j -> p j e")
+                    if eng == "S":
+                        nc.scalar.copy(dst, src)
+                    else:
+                        nc.vector.tensor_copy(dst, src)
+            elif kind == "Q":
+                a, j0, j1 = step[1:]
+                nc.vector.quantize_mx(
+                    out=x_codes(a, j0, j1).bitcast(FP8X4),
+                    scales=x_scales(a, j0, j1),
+                    in_=x_bf(a, j0, j1).rearrange("p j t -> p (j t)"),
+                )
+            elif kind == "g":
+                half, t, a, bank = step[1:]
+                if a == 0:
+                    held[("g", half, t)] = bank_tile(bank)
+                first_layer_pass(held[("g", half, t)][:], 0, a, t, slice(512 * half, 512 * half + 512))
+            elif kind == "s":
+                half, t, j0, j1 = step[1:]
+                nc.scalar.activation(
+                    gate[:, j0 // 128 : j1 // 128, t, :],
+                    held[("g", half, t)][:, j0 - 512 * half : j1 - 512 * half].rearrange("p (c j) -> p c j", j=128),
+                    ACT.Silu,
+                )
+            elif kind == "u":
+                c, bank = step[1:]
+                held[("u", c)] = bank_tile(bank)
+                for t in range(4):
+                    for a in range(2):
+                        first_layer_pass(
+                            held[("u", c)][:, 128 * t : 128 * t + 128], 1, a, t, slice(128 * c, 128 * c + 128)
+                        )
+            elif kind == "m":
+                c = step[1]
+                cols = slice(128 * c, 128 * c + 128)
+                nc.vector.tensor_tensor(
+                    h_bf[:, cols, :].rearrange("p (c i) t -> p c t i", i=4),
+                    held[("u", c)][:].rearrange("p (t c i) -> p c t i", t=4, i=4),
+                    gate[:, c].rearrange("p t (c i) -> p c t i", i=4),
+                    ALU.mult,
+                )
+            elif kind == "qh":
+                j0, j1 = step[1:]
+                nc.vector.quantize_mx(
+                    out=h_codes[:, j0:j1].bitcast(FP8X4),
+                    scales=h_scales[:, j0:j1],
+                    in_=h_bf[:, j0:j1, :].rearrange("p j t -> p (j t)"),
+                )
+            elif kind == "y":
+                j0, j1, tiles, bank = step[1:]
+                width = j1 - j0
+                acc = bank_tile(bank)
+                held[("y", j0, tiles)] = (acc, j1)
+                for n, c in enumerate(tiles):
+                    nc.tensor.matmul_mx(
+                        out=acc[:, n * width : (n + 1) * width],
+                        lhsT=wd_sb[:, 256 * c : 256 * c + 256].bitcast(FP4X4),
+                        lhsT_scale=sd_sb[:, 128 * c : 128 * c + 128],
+                        rhs=h_codes[:, j0:j1].bitcast(FP8X4),
+                        rhs_scale=h_scales[:, j0:j1],
+                        start=True,
+                        stop=True,
+                    )
+            elif kind == "b":
+                j0, tiles, eng = step[1:]
+                acc, j1 = held[("y", j0, tiles)]
+                width = j1 - j0
+                if j0 not in y_sb:
+                    y_sb[j0] = keep.tile([P, 4, width], F32, name="y_sb%d" % j0)
+                if eng == "S":
+                    for n, c in enumerate(tiles):
+                        nc.scalar.activation(
+                            y_sb[j0][:, c, :], acc[:, n * width : (n + 1) * width], ACT.Identity, bias=b_sb[:, c : c + 1]
+                        )
+                else:
+                    c0, c1 = tiles[0], tiles[-1] + 1
+                    nc.vector.tensor_tensor(
+                        y_sb[j0][:, c0:c1, :],
+                        acc[:, 0 : (c1 - c0) * width].rearrange("p (c j) -> p c j", j=width),
+                        b_sb[:, c0:c1].unsqueeze(2).to_broadcast([P, c1 - c0, width]),
+                        ALU.add,
+                    )
+            elif kind == "st":
+                j0, j1, tiles = step[1:]
+                c0, c1 = tiles[0], tiles[-1] + 1
+                nc.sync.dma_start(out=out_v[:, c0:c1, j0:j1], in_=y_sb[j0][:, c0:c1, :])

@@ -1,6 +1,7 @@
 from contextlib import ExitStack
 
 import concourse.mybir as mybir
+from concourse.masks import make_identity
 
 K, R, N, T, J = 1024, 512, 512, 2048, 1024
 FLOPS = 2 * (2 * K * R + R * N) * J
@@ -36,101 +37,112 @@ PLAN = [
     ('I', 2, 0, 512, 'S'),
     ('G', 5, 512, 1024),
     ('I', 2, 512, 1024, 'S'),
-    ('G', 7, 0, 128),
     ('G', 6, 0, 512),
+    ('G', 7, 0, 128),
     ('G', 7, 128, 256),
     ('I', 3, 128, 256, 'S'),
     ('G', 7, 256, 512),
     ('Q', 0, 0, 512),
+    ('g', 0, 0, 0, 3),
     ('Q', 1, 128, 256),
+    ('I', 3, 0, 128, 'S'),
     ('I', 3, 256, 512, 'S'),
     ('g', 0, 1, 0, 0),
-    ('g', 0, 3, 0, 6),
-    ('I', 3, 0, 128, 'S'),
+    ('g', 0, 2, 0, 4),
     ('Q', 1, 0, 128),
     ('Q', 1, 256, 512),
-    ('g', 0, 0, 0, 7),
-    ('g', 0, 3, 1, 3),
+    ('g', 0, 3, 0, 5),
     ('g', 0, 0, 1, 0),
-    ('g', 0, 1, 1, 1),
-    ('s', 0, 0, 256, 512),
-    ('g', 0, 2, 0, 3),
-    ('G', 6, 512, 768),
-    ('Q', 0, 512, 1024),
-    ('s', 0, 0, 0, 256),
-    ('g', 0, 2, 1, 2),
-    ('u', 2, 7),
-    ('G', 7, 768, 1024),
-    ('s', 0, 2, 0, 256),
-    ('u', 1, 5),
-    ('s', 0, 3, 0, 256),
-    ('s', 0, 2, 256, 512),
-    ('s', 0, 1, 0, 256),
-    ('m', 1),
-    ('s', 0, 1, 256, 512),
-    ('g', 1, 3, 0, 5),
-    ('G', 7, 512, 768),
-    ('u', 0, 4),
-    ('I', 3, 512, 768, 'V'),
-    ('s', 0, 3, 256, 512),
-    ('m', 0),
     ('G', 6, 768, 1024),
-    ('u', 3, 2),
-    ('I', 3, 768, 1024, 'S'),
+    ('g', 0, 1, 1, 0),
+    ('G', 6, 512, 768),
+    ('u', 0, 2),
+    ('s', 0, 0, 256, 512),
+    ('s', 0, 1, 0, 256),
+    ('G', 7, 512, 768),
+    ('s', 0, 1, 256, 512),
+    ('s', 0, 0, 0, 256),
+    ('Q', 0, 512, 1024),
+    ('G', 7, 768, 1024),
+    ('g', 0, 2, 1, 0),
+    ('u', 1, 0),
+    ('u', 3, 7),
+    ('g', 1, 1, 0, 1),
+    ('I', 3, 768, 1024, 'V'),
     ('Q', 1, 768, 1024),
-    ('g', 1, 2, 0, 1),
-    ('m', 2),
-    ('g', 1, 1, 0, 3),
-    ('g', 1, 0, 0, 0),
-    ('qh', 0, 256),
-    ('Q', 1, 512, 768),
-    ('g', 1, 3, 1, 3),
+    ('g', 0, 3, 1, 0),
+    ('s', 0, 2, 256, 512),
+    ('s', 0, 2, 0, 256),
+    ('u', 2, 3),
+    ('s', 0, 3, 256, 512),
+    ('g', 1, 0, 0, 6),
+    ('g', 1, 3, 0, 4),
+    ('s', 0, 3, 0, 256),
+    ('I', 3, 512, 768, 'V'),
     ('m', 3),
-    ('s', 1, 3, 512, 1024),
-    ('qh', 256, 512),
-    ('y', 0, 256, (0, 1), 7),
+    ('Q', 1, 512, 768),
+    ('m', 0),
+    ('g', 1, 3, 1, 3),
+    ('m', 2),
+    ('g', 1, 1, 1, 1),
+    ('g', 1, 2, 0, 7),
+    ('s', 1, 3, 512, 768),
     ('g', 1, 2, 1, 2),
-    ('b', 0, (0, 1), 'S'),
-    ('y', 256, 512, (2, 3), 2),
-    ('g', 1, 0, 1, 4),
-    ('g', 1, 1, 1, 5),
-    ('b', 256, (2, 3), 'S'),
-    ('s', 1, 2, 512, 1024),
-    ('s', 1, 0, 512, 1024),
-    ('y', 0, 256, (2, 3), 4),
-    ('u', 4, 1),
-    ('u', 7, 6),
-    ('s', 1, 1, 512, 1024),
-    ('m', 4),
-    ('m', 7),
-    ('y', 256, 512, (0, 1), 7),
-    ('u', 5, 5),
-    ('b', 0, (2, 3), 'S'),
-    ('m', 5),
-    ('qh', 896, 1024),
-    ('u', 6, 0),
-    ('y', 896, 1024, (2, 3), 1),
-    ('b', 256, (0, 1), 'S'),
-    ('st', 256, 512, (0, 1, 2, 3)),
+    ('g', 1, 0, 1, 0),
+    ('s', 1, 1, 768, 1024),
+    ('s', 1, 0, 512, 768),
+    ('s', 1, 0, 768, 1024),
+    ('s', 1, 3, 768, 1024),
+    ('s', 1, 2, 768, 1024),
+    ('u', 6, 2),
+    ('u', 7, 5),
     ('m', 6),
+    ('qh', 256, 512),
+    ('m', 1),
     ('qh', 768, 896),
-    ('b', 896, (2, 3), 'S'),
+    ('qh', 0, 256),
+    ('s', 1, 2, 512, 768),
+    ('y', 0, 256, (2, 3), 3),
+    ('y', 256, 512, (2, 3), 4),
+    ('y', 256, 512, (0, 1), 0),
+    ('b', 256, (2, 3), 'S'),
+    ('y', 0, 256, (0, 1), 6),
+    ('s', 1, 1, 512, 768),
+    ('b', 256, (0, 1), 'V'),
+    ('u', 4, 1),
+    ('u', 5, 2),
+    ('m', 7),
+    ('qh', 896, 1024),
+    ('y', 768, 896, (2, 3), 0),
+    ('b', 768, (2, 3), 'S'),
+    ('m', 4),
+    ('m', 5),
     ('qh', 512, 768),
-    ('st', 896, 1024, (2, 3)),
-    ('y', 768, 896, (0, 1, 2, 3), 4),
-    ('b', 768, (0, 1, 2, 3), 'V'),
-    ('y', 512, 768, (0, 1), 6),
+    ('y', 512, 768, (0, 1), 1),
+    ('b', 0, (2, 3), 'S'),
+    ('st', 256, 512, (2, 3)),
+    ('y', 512, 768, (2, 3), 3),
     ('b', 512, (0, 1), 'S'),
-    ('y', 896, 1024, (0, 1), 3),
-    ('b', 896, (0, 1), 'S'),
-    ('y', 512, 768, (2, 3), 7),
-    ('b', 512, (2, 3), 'V'),
-    ('st', 768, 896, (0, 1, 2, 3)),
-    ('st', 0, 256, (0, 1, 2, 3)),
-    ('st', 512, 768, (0, 1, 2, 3)),
+    ('b', 0, (0, 1), 'S'),
+    ('st', 0, 256, (2, 3)),
+    ('y', 768, 896, (0, 1), 5),
+    ('y', 896, 1024, (2, 3), 4),
+    ('b', 768, (0, 1), 'V'),
+    ('y', 896, 1024, (0, 1), 2),
+    ('st', 768, 896, (2, 3)),
+    ('b', 896, (0, 1), 'V'),
+    ('b', 512, (2, 3), 'S'),
+    ('b', 896, (2, 3), 'S'),
     ('st', 896, 1024, (0, 1)),
+    ('st', 768, 896, (0, 1)),
+    ('st', 0, 256, (0, 1)),
+    ('st', 256, 512, (0, 1)),
+    ('st', 896, 1024, (2, 3)),
+    ('st', 512, 768, (0, 1)),
+    ('st', 512, 768, (2, 3)),
 ]
-SHARES = {"x_codes0_0": "plane5", "x_codes0_512": "x_bf1_256", "picked3_512": "x_bf1_128", "picked3_768": "x_bf1_0"}
+SHARES = {'x_codes0_0': 'plane5', 'x_codes0_512': 'x_bf1_0', 'picked3_768': 'x_bf1_256', 'picked3_512': 'x_bf1_128', 'y_sb768_0': 'h_bf512'}
+H_STRETCHES = ((0, 256), (256, 512), (512, 768), (768, 896), (896, 1024))
 STRETCHES = ((0, 128), (128, 256), (256, 512), (512, 768), (768, 1024))
 
 
@@ -180,11 +192,22 @@ def tile_list_silu_bias_kernel(
             lo = j0 // 512 * 512
             return tile_of("x_scales%d_%d" % (a, lo), [P, 512], U8)[:, j0 - lo : j1 - lo]
 
-        gate = keep.tile([P, 8, 4, 128], F32, name="gate")
-        h_bf = keep.tile([P, J, 4], BF16, name="h_bf", align_bytes=64)
-        h_codes = keep.tile([P, J], U32, name="h_codes", align_bytes=64)
-        h_scales = keep.tile([P, J], U8, name="h_scales", align_bytes=64)
-        y_sb = {}
+        def gate(j0):
+            return tile_of("gate%d" % (j0 // 256), [P, 2, 4, 128], F32)
+
+        def h_bf(j0, j1):
+            lo, hi = [s for s in H_STRETCHES if s[0] <= j0 < s[1]][0]
+            return tile_of("h_bf%d" % lo, [P, hi - lo, 4], BF16)[:, j0 - lo : j1 - lo, :]
+
+        def h_codes(j0, j1):
+            return tile_of("h_codes%d" % j0, [P, j1 - j0], U32)[:]
+
+        def h_scales(j0, j1):
+            return tile_of("h_scales%d" % j0, [P, j1 - j0], U8)[:]
+
+        def y_sb(j0, j1, c0):
+            return tile_of("y_sb%d_%d" % (j0, c0), [P, 2, j1 - j0], F32)
+
         warm = keep.tile([P, 2], F32, name="warm")
 
         nc.vector.memset(s_raw[0][:].rearrange("p a n -> p (a n)").bitcast(I32), 0)
@@ -223,14 +246,18 @@ def tile_list_silu_bias_kernel(
                 in_=s_raw[w][:].rearrange("p a (m t) -> p a t m", t=4),
             )
 
+        wgt_rows = keep.tile([P, P], F32, name="wgt_rows")
+        wgt_wide = keep.tile([P, 8, P], F32, name="wgt_wide")
+        ident = keep.tile([P, P], F32, name="ident")
+        make_identity(nc, ident[:])
+
         nc.sync.dma_start(offsets[:], offs)
+        nc.sync.dma_start(out=wgt_rows[:], in_=wgt.rearrange("(g r) (c j) -> g (r c) j", r=16, j=P)[:, 0:16, :])
         load_words(0, wg_words)
         load_words(1, wu_words)
         load_scales(s_raw[0], wg_scales)
-        nc.sync.dma_start(out=wgt_sb[0][:], in_=wgt[:, 0:512])
         load_plane(0)
         load_scales(s_raw[1], wu_scales)
-        nc.sync.dma_start(out=wgt_sb[1][:], in_=wgt[:, 512:1024])
         for q in range(1, 8):
             load_plane(q)
         nc.sync.dma_start(out=wd_sb[:].bitcast(I32), in_=wd_words[0].bitcast(I32))
@@ -249,6 +276,20 @@ def tile_list_silu_bias_kernel(
 
         def bank_tile(bank):
             return psum.tile([P, 512], F32, name="bank%d" % bank)
+
+        turned = bank_tile(0)
+        nc.tensor.transpose(turned[:, 0:P], wgt_rows[:], ident[:])
+        for h in range(2):
+            src = turned[:, 0:P].rearrange("j (q c) -> j c q", c=8)[:, 4 * h : 4 * h + 4, :]
+            nc.scalar.copy(
+                wgt_wide[:, 4 * h : 4 * h + 4, :].rearrange("j c (q i) -> j c q i", i=8),
+                src.unsqueeze(3).to_broadcast([P, 4, 16, 8]),
+            )
+        for h in range(2):
+            back = bank_tile(1 + h)
+            for c in range(4):
+                nc.tensor.transpose(back[:, c * P : (c + 1) * P], wgt_wide[:, 4 * h + c, :], ident[:])
+            nc.scalar.copy(wgt_sb[h][:], back[:])
 
         def first_layer_pass(dst, w, a, t, cols):
             nc.tensor.matmul_mx(
@@ -299,7 +340,7 @@ def tile_list_silu_bias_kernel(
             elif kind == "s":
                 half, t, j0, j1 = step[1:]
                 nc.scalar.activation(
-                    gate[:, j0 // 128 : j1 // 128, t, :],
+                    gate(j0)[:, :, t, :],
                     held[("g", half, t)][:, j0 - 512 * half : j1 - 512 * half].rearrange("p (c j) -> p c j", j=128),
                     ACT.Silu,
                 )
@@ -315,17 +356,17 @@ def tile_list_silu_bias_kernel(
                 c = step[1]
                 cols = slice(128 * c, 128 * c + 128)
                 nc.vector.tensor_tensor(
-                    h_bf[:, cols, :].rearrange("p (c i) t -> p c t i", i=4),
+                    h_bf(cols.start, cols.stop).rearrange("p (c i) t -> p c t i", i=4),
                     held[("u", c)][:].rearrange("p (t c i) -> p c t i", t=4, i=4),
-                    gate[:, c].rearrange("p t (c i) -> p c t i", i=4),
+                    gate(cols.start)[:, c % 2].rearrange("p t (c i) -> p c t i", i=4),
                     ALU.mult,
                 )
             elif kind == "qh":
                 j0, j1 = step[1:]
                 nc.vector.quantize_mx(
-                    out=h_codes[:, j0:j1].bitcast(FP8X4),
-                    scales=h_scales[:, j0:j1],
-                    in_=h_bf[:, j0:j1, :].rearrange("p j t -> p (j t)"),
+                    out=h_codes(j0, j1).bitcast(FP8X4),
+                    scales=h_scales(j0, j1),
+                    in_=h_bf(j0, j1).rearrange("p j t -> p (j t)"),
                 )
             elif kind == "y":
                 j0, j1, tiles, bank = step[1:]
@@ -337,8 +378,8 @@ def tile_list_silu_bias_kernel(
                         out=acc[:, n * width : (n + 1) * width],
                         lhsT=wd_sb[:, 256 * c : 256 * c + 256].bitcast(FP4X4),
                         lhsT_scale=sd_sb[:, 128 * c : 128 * c + 128],
-                        rhs=h_codes[:, j0:j1].bitcast(FP8X4),
-                        rhs_scale=h_scales[:, j0:j1],
+                        rhs=h_codes(j0, j1).bitcast(FP8X4),
+                        rhs_scale=h_scales(j0, j1),
                         start=True,
                         stop=True,
                     )
@@ -346,17 +387,15 @@ def tile_list_silu_bias_kernel(
                 j0, tiles, eng = step[1:]
                 acc, j1 = held[("y", j0, tiles)]
                 width = j1 - j0
-                if j0 not in y_sb:
-                    y_sb[j0] = keep.tile([P, 4, width], F32, name="y_sb%d" % j0)
                 if eng == "S":
                     for n, c in enumerate(tiles):
                         nc.scalar.activation(
-                            y_sb[j0][:, c, :], acc[:, n * width : (n + 1) * width], ACT.Identity, bias=b_sb[:, c : c + 1]
+                            y_sb(j0, j1, tiles[0])[:, n, :], acc[:, n * width : (n + 1) * width], ACT.Identity, bias=b_sb[:, c : c + 1]
                         )
                 else:
                     c0, c1 = tiles[0], tiles[-1] + 1
                     nc.vector.tensor_tensor(
-                        y_sb[j0][:, c0:c1, :],
+                        y_sb(j0, j1, c0)[:],
                         acc[:, 0 : (c1 - c0) * width].rearrange("p (c j) -> p c j", j=width),
                         b_sb[:, c0:c1].unsqueeze(2).to_broadcast([P, c1 - c0, width]),
                         ALU.add,
@@ -364,4 +403,4 @@ def tile_list_silu_bias_kernel(
             elif kind == "st":
                 j0, j1, tiles = step[1:]
                 c0, c1 = tiles[0], tiles[-1] + 1
-                nc.sync.dma_start(out=out_v[:, c0:c1, j0:j1], in_=y_sb[j0][:, c0:c1, :])
+                nc.sync.dma_start(out=out_v[:, c0:c1, j0:j1], in_=y_sb(j0, j1, c0)[:])

@@ -319,8 +319,8 @@ def tile_list_silu_bias_kernel(
                 a, e = divmod(pair, 2)
                 parts = [s for s in STRETCHES if j0 <= s[0] < j1] if a == 1 else [(j0, j1)]
                 for lo, hi in parts:
-                    dst = x_bf(a, lo, hi)[:, :, 2 * e : 2 * e + 2]
-                    src = picked(pair, lo, hi).rearrange("p e j -> p j e")
+                    dst = x_bf(a, lo, hi)[:, :, 2 * e : 2 * e + 2].rearrange("p (c i) e -> p c e i", i=2)
+                    src = picked(pair, lo, hi).rearrange("p e (c i) -> p c e i", i=2)
                     if eng == "S":
                         nc.scalar.copy(dst, src)
                     else:
@@ -356,9 +356,9 @@ def tile_list_silu_bias_kernel(
                 c = step[1]
                 cols = slice(128 * c, 128 * c + 128)
                 nc.vector.tensor_tensor(
-                    h_bf(cols.start, cols.stop).rearrange("p (c i) t -> p c t i", i=4),
-                    held[("u", c)][:].rearrange("p (t c i) -> p c t i", t=4, i=4),
-                    gate(cols.start)[:, c % 2].rearrange("p t (c i) -> p c t i", i=4),
+                    h_bf(cols.start, cols.stop).rearrange("p (c i) t -> p c t i", i=2),
+                    held[("u", c)][:].rearrange("p (t c i) -> p c t i", t=4, i=2),
+                    gate(cols.start)[:, c % 2].rearrange("p t (c i) -> p c t i", i=2),
                     ALU.mult,
                 )
             elif kind == "qh":

from contextlib import ExitStack

import concourse.mybir as mybir
from concourse.masks import make_identity

K, R, N, T, J = 1024, 512, 512, 2048, 1024
FLOPS = 2 * (2 * K * R + R * N) * J

F32 = mybir.dt.float32
BF16 = mybir.dt.bfloat16
I32 = mybir.dt.int32
U32 = mybir.dt.uint32
U16 = mybir.dt.uint16
U8 = mybir.dt.uint8
FP8X4 = mybir.dt.float8_e4m3fn_x4
FP4X4 = mybir.dt.float4_e2m1fn_x4
ACT = mybir.ActivationFunctionType
ALU = mybir.AluOpType

P = 128
PLAN = [
    ('G', 0, 0, 512),
    ('G', 0, 512, 1024),
    ('G', 1, 0, 512),
    ('I', 0, 0, 512, 'S'),
    ('G', 1, 512, 1024),
    ('I', 0, 512, 1024, 'S'),
    ('G', 2, 0, 512),
    ('G', 2, 512, 1024),
    ('G', 3, 0, 512),
    ('I', 1, 0, 512, 'S'),
    ('G', 3, 512, 1024),
    ('I', 1, 512, 1024, 'S'),
    ('G', 4, 0, 512),
    ('G', 4, 512, 1024),
    ('G', 5, 0, 512),
    ('I', 2, 0, 512, 'S'),
    ('G', 5, 512, 1024),
    ('I', 2, 512, 1024, 'S'),
    ('G', 6, 0, 512),
    ('G', 7, 0, 128),
    ('G', 7, 128, 256),
    ('I', 3, 128, 256, 'S'),
    ('G', 7, 256, 512),
    ('Q', 0, 0, 512),
    ('g', 0, 0, 0, 3),
    ('Q', 1, 128, 256),
    ('I', 3, 0, 128, 'S'),
    ('I', 3, 256, 512, 'S'),
    ('g', 0, 1, 0, 0),
    ('g', 0, 2, 0, 4),
    ('Q', 1, 0, 128),
    ('Q', 1, 256, 512),
    ('g', 0, 3, 0, 5),
    ('g', 0, 0, 1, 0),
    ('G', 6, 768, 1024),
    ('g', 0, 1, 1, 0),
    ('G', 6, 512, 768),
    ('u', 0, 2),
    ('s', 0, 0, 256, 512),
    ('s', 0, 1, 0, 256),
    ('G', 7, 512, 768),
    ('s', 0, 1, 256, 512),
    ('s', 0, 0, 0, 256),
    ('Q', 0, 512, 1024),
    ('G', 7, 768, 1024),
    ('g', 0, 2, 1, 0),
    ('u', 1, 0),
    ('u', 3, 7),
    ('g', 1, 1, 0, 1),
    ('I', 3, 768, 1024, 'V'),
    ('Q', 1, 768, 1024),
    ('g', 0, 3, 1, 0),
    ('s', 0, 2, 256, 512),
    ('s', 0, 2, 0, 256),
    ('u', 2, 3),
    ('s', 0, 3, 256, 512),
    ('g', 1, 0, 0, 6),
    ('g', 1, 3, 0, 4),
    ('s', 0, 3, 0, 256),
    ('I', 3, 512, 768, 'V'),
    ('m', 3),
    ('Q', 1, 512, 768),
    ('m', 0),
    ('g', 1, 3, 1, 3),
    ('m', 2),
    ('g', 1, 1, 1, 1),
    ('g', 1, 2, 0, 7),
    ('s', 1, 3, 512, 768),
    ('g', 1, 2, 1, 2),
    ('g', 1, 0, 1, 0),
    ('s', 1, 1, 768, 1024),
    ('s', 1, 0, 512, 768),
    ('s', 1, 0, 768, 1024),
    ('s', 1, 3, 768, 1024),
    ('s', 1, 2, 768, 1024),
    ('u', 6, 2),
    ('u', 7, 5),
    ('m', 6),
    ('qh', 256, 512),
    ('m', 1),
    ('qh', 768, 896),
    ('qh', 0, 256),
    ('s', 1, 2, 512, 768),
    ('y', 0, 256, (2, 3), 3),
    ('y', 256, 512, (2, 3), 4),
    ('y', 256, 512, (0, 1), 0),
    ('b', 256, (2, 3), 'S'),
    ('y', 0, 256, (0, 1), 6),
    ('s', 1, 1, 512, 768),
    ('b', 256, (0, 1), 'V'),
    ('u', 4, 1),
    ('u', 5, 2),
    ('m', 7),
    ('qh', 896, 1024),
    ('y', 768, 896, (2, 3), 0),
    ('b', 768, (2, 3), 'S'),
    ('m', 4),
    ('m', 5),
    ('qh', 512, 768),
    ('y', 512, 768, (0, 1), 1),
    ('b', 0, (2, 3), 'S'),
    ('st', 256, 512, (2, 3)),
    ('y', 512, 768, (2, 3), 3),
    ('b', 512, (0, 1), 'S'),
    ('b', 0, (0, 1), 'S'),
    ('st', 0, 256, (2, 3)),
    ('y', 768, 896, (0, 1), 5),
    ('y', 896, 1024, (2, 3), 4),
    ('b', 768, (0, 1), 'V'),
    ('y', 896, 1024, (0, 1), 2),
    ('st', 768, 896, (2, 3)),
    ('b', 896, (0, 1), 'V'),
    ('b', 512, (2, 3), 'S'),
    ('b', 896, (2, 3), 'S'),
    ('st', 896, 1024, (0, 1)),
    ('st', 768, 896, (0, 1)),
    ('st', 0, 256, (0, 1)),
    ('st', 256, 512, (0, 1)),
    ('st', 896, 1024, (2, 3)),
    ('st', 512, 768, (0, 1)),
    ('st', 512, 768, (2, 3)),
]
SHARES = {'x_codes0_0': 'plane5', 'x_codes0_512': 'x_bf1_0', 'picked3_768': 'x_bf1_256', 'picked3_512': 'x_bf1_128', 'y_sb768_0': 'h_bf512'}
H_STRETCHES = ((0, 256), (256, 512), (512, 768), (768, 896), (896, 1024))
STRETCHES = ((0, 128), (128, 256), (256, 512), (512, 768), (768, 1024))


def tile_list_silu_bias_kernel(
    tc, xT, wgt, wg_words, wg_scales, wu_words, wu_scales, wd_words, wd_scales, b, offs, out
):
    nc = tc.nc
    with ExitStack() as ctx:
        keep = ctx.enter_context(tc.tile_pool(name="keep", bufs=1))
        psum = ctx.enter_context(tc.psum_pool(name="psum", bufs=1))

        offsets = keep.tile([P, J // 16], U16, name="offsets")
        w_raw = keep.tile([P, 4, 1024], U8, name="w_raw", align_bytes=64)
        s_raw = [keep.tile([P, 2, 512], U8, name="s_raw%d" % w, align_bytes=64) for w in range(2)]
        w_perm = keep.tile([P, 4, 4, 256], U8, name="w_perm", align_bytes=64)
        s_perm = keep.tile([P, 4, 4, 128], U8, name="s_perm", align_bytes=64)
        wd_sb = keep.tile([P, 1024], U8, name="wd_sb", align_bytes=64)
        sd_sb = keep.tile([P, 512], U8, name="sd_sb", align_bytes=64)
        b_sb = keep.tile([P, 4], F32, name="b_sb")
        made = {}

        def tile_of(name, shape, dtype):
            if name not in made:
                made[name] = keep.tile(shape, dtype, name=name, tag=SHARES.get(name, name), align_bytes=64)
            return made[name]

        wgt_sb = [tile_of("wgt%d" % h, [P, 512], F32) for h in range(2)]
        planes = [tile_of("plane%d" % q, [P, T], F32) for q in range(8)]

        def picked(pair, j0, j1):
            lo, hi = (j0 // 512 * 512, j0 // 512 * 512 + 512)
            if pair == 3 and j0 >= 512:
                lo, hi = (j0 // 256 * 256, j0 // 256 * 256 + 256)
            return tile_of("picked%d_%d" % (pair, lo), [P, 2, hi - lo], F32)[:, :, j0 - lo : j1 - lo]

        def x_bf(a, j0, j1):
            lo, hi = (j0 // 512 * 512, j0 // 512 * 512 + 512)
            if a == 1:
                lo, hi = [s for s in STRETCHES if s[0] <= j0 < s[1]][0]
            return tile_of("x_bf%d_%d" % (a, lo), [P, hi - lo, 4], BF16)[:, j0 - lo : j1 - lo, :]

        def x_codes(a, j0, j1):
            lo = j0 // 512 * 512
            return tile_of("x_codes%d_%d" % (a, lo), [P, 512], U32)[:, j0 - lo : j1 - lo]

        def x_scales(a, j0, j1):
            lo = j0 // 512 * 512
            return tile_of("x_scales%d_%d" % (a, lo), [P, 512], U8)[:, j0 - lo : j1 - lo]

        def gate(j0):
            return tile_of("gate%d" % (j0 // 256), [P, 2, 4, 128], F32)

        def h_bf(j0, j1):
            lo, hi = [s for s in H_STRETCHES if s[0] <= j0 < s[1]][0]
            return tile_of("h_bf%d" % lo, [P, hi - lo, 4], BF16)[:, j0 - lo : j1 - lo, :]

        def h_codes(j0, j1):
            return tile_of("h_codes%d" % j0, [P, j1 - j0], U32)[:]

        def h_scales(j0, j1):
            return tile_of("h_scales%d" % j0, [P, j1 - j0], U8)[:]

        def y_sb(j0, j1, c0):
            return tile_of("y_sb%d_%d" % (j0, c0), [P, 2, j1 - j0], F32)

        warm = keep.tile([P, 2], F32, name="warm")

        nc.vector.memset(s_raw[0][:].rearrange("p a n -> p (a n)").bitcast(I32), 0)
        nc.vector.memset(s_raw[1][:].rearrange("p a n -> p (a n)").bitcast(I32), 0)
        nc.vector.memset(sd_sb[:].bitcast(I32), 0)
        nc.vector.memset(warm[:, 0:1], 0.0)
        nc.scalar.activation(warm[:, 1:2], warm[:, 0:1], ACT.Silu)

        def load_words(w, words):
            nc.sync.dma_start(
                out=w_raw[:, 2 * w : 2 * w + 2, :].bitcast(I32),
                in_=words.rearrange("a p n -> p a n").bitcast(I32),
            )

        def load_scales(dst, scales):
            for q in range(4):
                nc.sync.dma_start(
                    out=dst[32 * q : 32 * q + 4].bitcast(I32),
                    in_=scales[:, 4 * q : 4 * q + 4, :].rearrange("a r n -> r a n").bitcast(I32),
                )

        def load_plane(q):
            a, i = divmod(q, 4)
            rows = xT[512 * a : 512 * a + 512, :].rearrange("(p i) t -> p i t", i=4)
            nc.sync.dma_start(out=planes[q][:], in_=rows[:, i, :])

        def permute_words(w):
            nc.vector.tensor_copy(
                out=w_perm[:, 2 * w : 2 * w + 2].bitcast(U16),
                in_=w_raw[:, 2 * w : 2 * w + 2, :].bitcast(U16).rearrange("p a (m t) -> p a t m", t=4),
            )

        def permute_scales(w):
            nc.vector.tensor_copy(
                out=s_perm[:, 2 * w : 2 * w + 2],
                in_=s_raw[w][:].rearrange("p a (m t) -> p a t m", t=4),
            )

        wgt_rows = keep.tile([P, P], F32, name="wgt_rows")
        wgt_wide = keep.tile([P, 8, P], F32, name="wgt_wide")
        ident = keep.tile([P, P], F32, name="ident")
        make_identity(nc, ident[:])

        nc.sync.dma_start(offsets[:], offs)
        nc.sync.dma_start(out=wgt_rows[:], in_=wgt.rearrange("(g r) (c j) -> g (r c) j", r=16, j=P)[:, 0:16, :])
        load_words(0, wg_words)
        load_words(1, wu_words)
        load_scales(s_raw[0], wg_scales)
        load_plane(0)
        load_scales(s_raw[1], wu_scales)
        for q in range(1, 8):
            load_plane(q)
        nc.sync.dma_start(out=wd_sb[:].bitcast(I32), in_=wd_words[0].bitcast(I32))
        for q in range(4):
            nc.sync.dma_start(
                out=sd_sb[32 * q : 32 * q + 4, :].bitcast(I32),
                in_=wd_scales[0, 4 * q : 4 * q + 4, :].bitcast(I32),
            )
        with nc.allow_non_contiguous_dma(reason="one bias value a partition"):
            nc.sync.dma_start(out=b_sb[:], in_=b.rearrange("(c p) -> p c", p=P))

        permute_words(0)
        permute_words(1)
        permute_scales(0)
        permute_scales(1)

        def bank_tile(bank):
            return psum.tile([P, 512], F32, name="bank%d" % bank)

        turned = bank_tile(0)
        nc.tensor.transpose(turned[:, 0:P], wgt_rows[:], ident[:])
        for h in range(2):
            src = turned[:, 0:P].rearrange("j (q c) -> j c q", c=8)[:, 4 * h : 4 * h + 4, :]
            nc.scalar.copy(
                wgt_wide[:, 4 * h : 4 * h + 4, :].rearrange("j c (q i) -> j c q i", i=8),
                src.unsqueeze(3).to_broadcast([P, 4, 16, 8]),
            )
        for h in range(2):
            back = bank_tile(1 + h)
            for c in range(4):
                nc.tensor.transpose(back[:, c * P : (c + 1) * P], wgt_wide[:, 4 * h + c, :], ident[:])
            nc.scalar.copy(wgt_sb[h][:], back[:])

        def first_layer_pass(dst, w, a, t, cols):
            nc.tensor.matmul_mx(
                out=dst,
                lhsT=w_perm[:, 2 * w + a, t, :].bitcast(FP4X4),
                lhsT_scale=s_perm[:, 2 * w + a, t, :],
                rhs=x_codes(a, cols.start, cols.stop).bitcast(FP8X4),
                rhs_scale=x_scales(a, cols.start, cols.stop),
                start=(a == 0),
                stop=(a == 1),
            )

        out_v = out.rearrange("(c p) j -> p c j", p=P)
        held = {}
        for step in PLAN:
            kind = step[0]
            if kind == "G":
                q, j0, j1 = step[1:]
                nc.vector.tensor_tensor(
                    picked(q // 2, j0, j1)[:, q % 2, :],
                    planes[q][:].indirect(offsets[:, j0 // 16 : j1 // 16]),
                    wgt_sb[j0 // 512][:, j0 % 512 : j0 % 512 + j1 - j0],
                    ALU.mult,
                )
            elif kind == "I":
                pair, j0, j1, eng = step[1:]
                a, e = divmod(pair, 2)
                parts = [s for s in STRETCHES if j0 <= s[0] < j1] if a == 1 else [(j0, j1)]
                for lo, hi in parts:
                    dst = x_bf(a, lo, hi)[:, :, 2 * e : 2 * e + 2].rearrange("p (c i) e -> p c e i", i=2)
                    src = picked(pair, lo, hi).rearrange("p e (c i) -> p c e i", i=2)
                    if eng == "S":
                        nc.scalar.copy(dst, src)
                    else:
                        nc.vector.tensor_copy(dst, src)
            elif kind == "Q":
                a, j0, j1 = step[1:]
                nc.vector.quantize_mx(
                    out=x_codes(a, j0, j1).bitcast(FP8X4),
                    scales=x_scales(a, j0, j1),
                    in_=x_bf(a, j0, j1).rearrange("p j t -> p (j t)"),
                )
            elif kind == "g":
                half, t, a, bank = step[1:]
                if a == 0:
                    held[("g", half, t)] = bank_tile(bank)
                first_layer_pass(held[("g", half, t)][:], 0, a, t, slice(512 * half, 512 * half + 512))
            elif kind == "s":
                half, t, j0, j1 = step[1:]
                nc.scalar.activation(
                    gate(j0)[:, :, t, :],
                    held[("g", half, t)][:, j0 - 512 * half : j1 - 512 * half].rearrange("p (c j) -> p c j", j=128),
                    ACT.Silu,
                )
            elif kind == "u":
                c, bank = step[1:]
                held[("u", c)] = bank_tile(bank)
                for t in range(4):
                    for a in range(2):
                        first_layer_pass(
                            held[("u", c)][:, 128 * t : 128 * t + 128], 1, a, t, slice(128 * c, 128 * c + 128)
                        )
            elif kind == "m":
                c = step[1]
                cols = slice(128 * c, 128 * c + 128)
                nc.vector.tensor_tensor(
                    h_bf(cols.start, cols.stop).rearrange("p (c i) t -> p c t i", i=2),
                    held[("u", c)][:].rearrange("p (t c i) -> p c t i", t=4, i=2),
                    gate(cols.start)[:, c % 2].rearrange("p t (c i) -> p c t i", i=2),
                    ALU.mult,
                )
            elif kind == "qh":
                j0, j1 = step[1:]
                nc.vector.quantize_mx(
                    out=h_codes(j0, j1).bitcast(FP8X4),
                    scales=h_scales(j0, j1),
                    in_=h_bf(j0, j1).rearrange("p j t -> p (j t)"),
                )
            elif kind == "y":
                j0, j1, tiles, bank = step[1:]
                width = j1 - j0
                acc = bank_tile(bank)
                held[("y", j0, tiles)] = (acc, j1)
                for n, c in enumerate(tiles):
                    nc.tensor.matmul_mx(
                        out=acc[:, n * width : (n + 1) * width],
                        lhsT=wd_sb[:, 256 * c : 256 * c + 256].bitcast(FP4X4),
                        lhsT_scale=sd_sb[:, 128 * c : 128 * c + 128],
                        rhs=h_codes(j0, j1).bitcast(FP8X4),
                        rhs_scale=h_scales(j0, j1),
                        start=True,
                        stop=True,
                    )
            elif kind == "b":
                j0, tiles, eng = step[1:]
                acc, j1 = held[("y", j0, tiles)]
                width = j1 - j0
                if eng == "S":
                    for n, c in enumerate(tiles):
                        nc.scalar.activation(
                            y_sb(j0, j1, tiles[0])[:, n, :], acc[:, n * width : (n + 1) * width], ACT.Identity, bias=b_sb[:, c : c + 1]
                        )
                else:
                    c0, c1 = tiles[0], tiles[-1] + 1
                    nc.vector.tensor_tensor(
                        y_sb(j0, j1, c0)[:],
                        acc[:, 0 : (c1 - c0) * width].rearrange("p (c j) -> p c j", j=width),
                        b_sb[:, c0:c1].unsqueeze(2).to_broadcast([P, c1 - c0, width]),
                        ALU.add,
                    )
            elif kind == "st":
                j0, j1, tiles = step[1:]
                c0, c1 = tiles[0], tiles[-1] + 1
                nc.sync.dma_start(out=out_v[:, c0:c1, j0:j1], in_=y_sb(j0, j1, c0)[:])
